import numpy as np
import ml_dtypes


def mxq(x, axis, fmt="e4m3"):
    dtype, down = {"e4m3": (ml_dtypes.float8_e4m3fn, 7), "e5m2": (ml_dtypes.float8_e5m2, 14)}[fmt]
    v = np.moveaxis(np.asarray(x, np.float32).astype(ml_dtypes.bfloat16).astype(np.float64), axis, -1)
    blocks = v.reshape(v.shape[:-1] + (-1, 32))
    amax = np.abs(blocks).max(-1, keepdims=True)
    byte = np.maximum(np.where(amax > 0, np.frexp(amax)[1] - 1 + 127, 0) - down, 1)
    scale = np.exp2(byte - 127.0)
    codes = (blocks / scale).astype(np.float32).astype(dtype).astype(np.float64)
    return np.moveaxis((codes * scale).reshape(v.shape), -1, axis)


WIDE = False


def mx_kscale(k):
    if not WIDE:
        return np.ones(k)
    levels = np.array([10, -10, 5, -5, 0])
    if k % 512:
        return np.exp2(np.random.permutation(np.resize(levels, k // 32))).repeat(32)
    a = np.empty((k // 512, 16))
    for p in range(k // 512):
        a[p, :8] = np.random.permutation(np.resize(levels, 8))
        for g in range(8):
            far = levels[np.abs(levels - a[p, g]) >= 10]
            a[p, g + 8] = far[np.random.randint(len(far))]
    return np.exp2(a.ravel()).repeat(32)


def f64(x):
    return np.asarray(x).astype(np.float64)


def striped(idx):
    return np.tile(idx.reshape(-1, 16).T, (8, 1)).astype(np.uint16)


def unstriped(offs):
    return offs[:16].T.reshape(-1).astype(np.int64)


def pack_weight(w):
    k, n = w.shape
    w = f64(np.asarray(w, np.float32).astype(ml_dtypes.bfloat16)).reshape(k // 32, 32, n)
    amax = np.abs(w).max(1)
    byte = np.clip(np.where(amax > 0, np.frexp(amax)[1] - 1 + 127 - 7, 1), 1, 254)
    scaled = (w * np.exp2(127.0 - byte)[:, None, :]).reshape(k, n).astype(np.float32)
    words = np.ascontiguousarray(scaled.reshape(k // 512, 128, 4, n).transpose(0, 1, 3, 2)).astype(ml_dtypes.float8_e4m3fn).view(np.uint8)
    return words, np.ascontiguousarray(byte.astype(np.uint8).reshape(k // 512, 16, n))


def unpack_weight(words, scales):
    g, p, n, _ = words.shape
    vals = np.ascontiguousarray(words).view(ml_dtypes.float8_e4m3fn).astype(np.float64) * np.repeat(np.exp2(scales.astype(np.float64) - 127.0), 8, axis=1)[..., None]
    return vals.transpose(0, 1, 3, 2).reshape(g * 512, n)


K, T, S, D, N, H, V, U = 512, 2048, 1024, 4, 256, 512, 256, 512


def setup_inputs():
    n = np.random.standard_normal
    s = mx_kscale(K)[:, None]
    u = mx_kscale(H)
    packed_xT = pack_weight(n((K, T)) * s)
    return {
        "x_words": packed_xT[0],
        "x_scales": packed_xT[1],
        "w1": (n((K, H)) / np.sqrt(K) / s).astype(np.float32),
        "w2": (n((K, H)) / np.sqrt(K) / s).astype(np.float32),
        "loc": (n((H, U))).astype(np.float32),
        "unit": (np.random.uniform(0.6, 1.4, (H, 1)) * u[:, None]).astype(np.float32),
        "w3": (n((H, N)) / np.sqrt(H) / u[:, None]).astype(np.float32),
        "offs": striped(np.random.permutation(T)[:S]),
        "gt": striped(np.random.permutation(np.concatenate([np.arange(V), np.random.randint(0, V, U - V)]))),
        "gs": striped(np.random.permutation(np.concatenate([np.arange(V), np.random.randint(0, V, U - V)]))),
    }


def reference(x_words, x_scales, w1, w2, loc, unit, w3, offs, gt, gs):
    xq = unpack_weight(x_words, x_scales)[:, unstriped(offs)]
    yg = mxq(f64(w2), 0, "e4m3").T @ xq
    w_ = np.exp(1.3 * np.tanh(yg))
    y = mxq(f64(w1), 0, "e4m3").T @ xq
    wy = w_ * y
    gist = (wy.reshape(len(wy), -1, D).sum(axis=2)) / (w_.reshape(len(w_), -1, D).sum(axis=2))
    g1 = gist[:, unstriped(gt)]
    g2 = gist[:, unstriped(gs)]
    zd = g1 - (0.6 * g2)
    hid = f64(unit) * (np.maximum(zd, f64(loc)))
    return mxq(f64(w3), 0, "e4m3").T @ mxq(hid, 0, "e4m3")

@@ -1,0 +1,305 @@
+from contextlib import ExitStack
+
+import concourse.mybir as mybir
+from concourse.masks import make_identity
+
+K, T, S, D, N, H, V, U = 512, 2048, 1024, 4, 256, 512, 256, 512
+FLOPS = 2 * K * H * S * 2 + 2 * H * N * U
+
+F32 = mybir.dt.float32
+BF16 = mybir.dt.bfloat16
+I32 = mybir.dt.int32
+U32 = mybir.dt.uint32
+U16 = mybir.dt.uint16
+U8 = mybir.dt.uint8
+FP8X4 = mybir.dt.float8_e4m3fn_x4
+ALU = mybir.AluOpType
+ACT = mybir.ActivationFunctionType
+
+P = 128
+PACK = 4
+SPARE = 16
+READER_CHUNKS = ((0, 256), (256, 512))
+SCALAR_BOTH = (0, 1)
+POOL_ADDS = (0, 1)
+FINISH_CHUNKS = ((0, 256), (256, 384), (384, 512))
+
+
+def tile_picked_ygistk_max_p_kernel(
+    tc, x_words, x_scales, w1, w2, loc, unit, w3, offs, gt, gs, out
+):
+    nc = tc.nc
+    with ExitStack() as ctx:
+        keep = ctx.enter_context(tc.tile_pool(name="keep", bufs=1))
+        ring = ctx.enter_context(tc.tile_pool(name="ring", bufs=2))
+        psum = ctx.enter_context(tc.psum_pool(name="psum", bufs=2))
+
+        offs_t = keep.tile([P, S // 16], U16, name="offs_t")
+        gt_t = keep.tile([P, U // 16], U16, name="gt_t")
+        gs_t = keep.tile([P, U // 16], U16, name="gs_t")
+        scale_win = keep.tile([P, T], U8, name="scale_win", align_bytes=64)
+        word_win = keep.tile([P, T], I32, name="word_win", align_bytes=64)
+        raw = {}
+        for name in ("w2", "w1"):
+            for c in range(2):
+                raw[name, c] = keep.tile([P, PACK, H // 2], F32, name="raw_%s_%d" % (name, c))
+        unit_t = keep.tile([P, PACK], F32, name="unit_t")
+        loc_t = keep.tile([P, PACK, U], F32, name="loc_t")
+        w3_raw = keep.tile([P, PACK, N], F32, name="w3_raw")
+        ident = keep.tile([P, P], F32, name="ident")
+        tables = [keep.tile([P, V + SPARE], F32, name="table%d" % t) for t in range(PACK)]
+
+        nc.vector.memset(scale_win[:].bitcast(I32), 0)
+        nc.sync.dma_start(offs_t[:], offs)
+        nc.sync.dma_start(out=unit_t[:], in_=unit.rearrange("(p j) o -> p (j o)", j=PACK))
+        for q in range(4):
+            nc.sync.dma_start(
+                out=scale_win[32 * q : 32 * q + 4, :].bitcast(I32),
+                in_=x_scales[0, 4 * q : 4 * q + 4, :].bitcast(I32),
+            )
+
+        def load_half(name, w, c):
+            cols = w[:, c * (H // 2) : (c + 1) * (H // 2)]
+            nc.sync.dma_start(out=raw[name, c][:], in_=cols.rearrange("(p j) c -> p j c", j=PACK))
+
+        nc.sync.dma_start(out=word_win[:], in_=x_words[0].rearrange("p n t -> p (n t)").bitcast(I32))
+        load_half("w2", w2, 0)
+        load_half("w2", w2, 1)
+        load_half("w1", w1, 0)
+        load_half("w1", w1, 1)
+        nc.sync.dma_start(out=w3_raw[:], in_=w3.rearrange("(p j) m -> p j m", j=PACK))
+        nc.sync.dma_start(gs_t[:], gs)
+        nc.sync.dma_start(gt_t[:], gt)
+        nc.sync.dma_start(out=loc_t[:], in_=loc.rearrange("(p j) r -> p j r", j=PACK))
+
+        make_identity(nc, ident[:])
+        for t in range(PACK):
+            nc.gpsimd.memset(tables[t][:, V:], 0.0)
+
+        x_sc = [keep.tile([P, D, P], U8, name="x_sc%d" % h, align_bytes=64) for h in range(2)]
+        x_w = [keep.tile([P, D, P], U32, name="x_w%d" % h, align_bytes=64) for h in range(2)]
+
+        def gather_scales(h):
+            nc.vector.tensor_copy(
+                out=x_sc[h][:].rearrange("p d v -> p v d"),
+                in_=scale_win[:].indirect(offs_t[:, 32 * h : 32 * (h + 1)]),
+            )
+
+        def gather_words(h):
+            nc.vector.tensor_copy(
+                out=x_w[h][:].rearrange("p d v -> p v d"),
+                in_=word_win[:].bitcast(U32).indirect(offs_t[:, 32 * h : 32 * (h + 1)]),
+            )
+
+        rounded, codes, scales = {}, {}, {}
+        for name in ("w2", "w1"):
+            rounded[name] = keep.tile([P, PACK, P, PACK], BF16, name="rounded_" + name, align_bytes=64)
+
+        def round_part(copy, name, c, m0, m1):
+            copy(
+                out=rounded[name][:, :, 64 * c + m0 : 64 * c + m1, :].rearrange("p t m j -> p m j t"),
+                in_=raw[name, c][:, :, PACK * m0 : PACK * m1].rearrange("p j (m t) -> p m j t", t=PACK),
+            )
+
+        def quantize_tiles(name, t0, t1):
+            code = keep.tile([P, t1 - t0, P], U32, name="codes_%s_%d" % (name, t0), align_bytes=64)
+            scale = keep.tile([P, t1 - t0, P], U8, name="scales_%s_%d" % (name, t0), align_bytes=64)
+            nc.vector.quantize_mx(
+                out=code[:].rearrange("p t m -> p (t m)").bitcast(FP8X4),
+                scales=scale[:].rearrange("p t m -> p (t m)"),
+                in_=rounded[name][:, t0:t1, :, :].rearrange("p t m j -> p (t m j)"),
+            )
+            for t in range(t0, t1):
+                codes[name, t] = code[:, t - t0, :]
+                scales[name, t] = scale[:, t - t0, :]
+
+        def product(name, t, h, tag):
+            bank = psum.tile([P, D, P], F32, name=tag)
+            for d in range(D):
+                nc.tensor.matmul_mx(
+                    out=bank[:, d, :],
+                    lhsT=x_w[h][:, d, :].bitcast(FP8X4),
+                    lhsT_scale=x_sc[h][:, d, :],
+                    rhs=codes[name, t].bitcast(FP8X4),
+                    rhs_scale=scales[name, t],
+                    start=True,
+                    stop=True,
+                )
+            return bank
+
+        weight, weighted = {}, {}
+
+        def make_weights(t, h):
+            bank = product("w2", t, h, "gate_bank")
+            squashed = ring.tile([P, D, P], F32, name="squashed")
+            nc.scalar.activation(squashed[:], bank[:], ACT.Tanh)
+            weight[t, h] = keep.tile([P, D, P], F32, name="weight%d%d" % (t, h))
+            nc.scalar.activation(weight[t, h][:], squashed[:], ACT.Exp, scale=1.3)
+
+        def weigh_values(t, h):
+            bank = product("w1", t, h, "value_bank")
+            weighted[t, h] = keep.tile([P, D, P], F32, name="weighted%d%d" % (t, h))
+            nc.vector.tensor_tensor(weighted[t, h][:], bank[:], weight[t, h][:], ALU.mult)
+
+        def sum_members(bank, terms, h):
+            for d in range(D):
+                nc.tensor.matmul(
+                    out=bank[:, h, :],
+                    lhsT=terms[:, d, :],
+                    rhs=ident[:],
+                    is_transpose=True,
+                    start=(d == 0),
+                    stop=(d == D - 1),
+                )
+
+        sign = keep.tile([P, PACK], F32, name="sign")
+        size = keep.tile([P, PACK], F32, name="size")
+        loc_s = keep.tile([P, PACK, U], F32, name="loc_s")
+        w3_signed = keep.tile([P, PACK, N], F32, name="w3_signed")
+        w3_rounded = keep.tile([P, N, PACK], BF16, name="w3_rounded", align_bytes=64)
+        w3_codes = keep.tile([P, N], U32, name="w3_codes", align_bytes=64)
+        w3_scales = keep.tile([P, N], U8, name="w3_scales", align_bytes=64)
+
+        def split_unit():
+            step = keep.tile([P, PACK], F32, name="step")
+            nc.gpsimd.tensor_scalar(step[:], unit_t[:], 0.0, 2.0, ALU.is_ge, ALU.mult)
+            nc.gpsimd.tensor_scalar(sign[:], step[:], 1.0, -1.0, ALU.mult, ALU.add)
+            nc.gpsimd.tensor_tensor(size[:], unit_t[:], sign[:], ALU.mult)
+
+        def scale_loc():
+            for t in range(PACK):
+                nc.gpsimd.tensor_scalar(loc_s[:, t, :], loc_t[:, t, :], size[:, t : t + 1], 0.0, ALU.mult, ALU.add)
+
+        def quantize_w3():
+            for j in range(PACK):
+                nc.gpsimd.tensor_scalar(w3_signed[:, j, :], w3_raw[:, j, :], sign[:, j : j + 1], 0.0, ALU.mult, ALU.add)
+            nc.gpsimd.tensor_copy(
+                out=w3_rounded[:].rearrange("p (c i) j -> p c j i", i=4),
+                in_=w3_signed[:].rearrange("p j (c i) -> p c j i", i=4),
+            )
+            nc.vector.quantize_mx(
+                out=w3_codes[:].bitcast(FP8X4), scales=w3_scales[:], in_=w3_rounded[:].rearrange("p m j -> p (m j)")
+            )
+
+        inverse = {}
+
+        pairs = {}
+
+        def pair_up(t, den_bank):
+            two = keep.tile([P, 2, P // 2], F32, name="two%d" % t)
+            nc.vector.tensor_reduce(
+                two[:].rearrange("p a v -> p (a v)"), den_bank.rearrange("p h v -> p v h"), mybir.AxisListType.X, ALU.mult
+            )
+            four = ring.tile([P, P // 2], F32, name="four")
+            nc.vector.tensor_reduce(four[:], two[:].rearrange("p a v -> p v a"), mybir.AxisListType.X, ALU.mult)
+            inv_four = ring.tile([P, 1, P // 2], F32, name="inv_four")
+            nc.vector.reciprocal(inv_four[:, 0, :], four[:])
+            inv_two = keep.tile([P, 1, P], F32, name="inv_two%d" % t)
+            nc.gpsimd.tensor_tensor(
+                inv_two[:, 0, :].rearrange("p (a v) -> p a v", a=2),
+                two[:, ::-1, :],
+                inv_four[:].to_broadcast([P, 2, P // 2]),
+                ALU.mult,
+            )
+            pairs[t] = inv_two
+
+        def invert(t, den_bank):
+            inv_two = pairs[t]
+            inverse[t] = keep.tile([P, 2, P], F32, name="inverse%d" % t)
+            nc.vector.tensor_tensor(inverse[t][:], den_bank[:, ::-1, :], inv_two[:].to_broadcast([P, 2, P]), ALU.mult)
+
+        def make_table(t, num_bank):
+            nc.vector.scalar_tensor_tensor(
+                tables[t][:, :V],
+                num_bank.rearrange("p h v -> p (h v)"),
+                size[:, t : t + 1],
+                inverse[t][:].rearrange("p h v -> p (h v)"),
+                ALU.mult,
+                ALU.mult,
+            )
+
+        diff = [keep.tile([P, PACK, r1 - r0], F32, name="diff%d" % r0) for r0, r1 in READER_CHUNKS]
+
+        def look_up(t, chunk):
+            r0, r1 = READER_CHUNKS[chunk]
+            other = keep.tile([P, r1 - r0], F32, name="other%d_%d" % (t, chunk))
+            nc.scalar.activation(other[:], tables[t][:].indirect(gs_t[:, r0 // 16 : r1 // 16]), ACT.Copy, scale=-0.6)
+            own = tables[t][:].indirect(gt_t[:, r0 // 16 : r1 // 16])
+            if t in SCALAR_BOTH:
+                fetched = keep.tile([P, r1 - r0], F32, name="fetched%d_%d" % (t, chunk))
+                nc.scalar.activation(fetched[:], own, ACT.Copy)
+                own = fetched[:]
+            adder = nc.gpsimd if t in POOL_ADDS else nc.vector
+            adder.tensor_tensor(diff[chunk][:, t, :], own, other[:], ALU.add)
+
+        def finish(chunk):
+            r0, r1 = FINISH_CHUNKS[chunk]
+            width = r1 - r0
+            half, c0 = divmod(r0, U // 2)
+            hid = keep.tile([P, width, PACK], BF16, name="hid%d" % chunk, align_bytes=64)
+            nc.vector.tensor_tensor(
+                hid[:].rearrange("p (c i) t -> p c t i", i=4),
+                diff[half][:, :, c0 : c0 + width].rearrange("p t (c i) -> p c t i", i=4),
+                loc_s[:, :, r0:r1].rearrange("p t (c i) -> p c t i", i=4),
+                ALU.max,
+            )
+            hid_codes = keep.tile([P, width], U32, name="hid_codes%d" % chunk, align_bytes=64)
+            hid_scales = keep.tile([P, width], U8, name="hid_scales%d" % chunk, align_bytes=64)
+            nc.vector.quantize_mx(
+                out=hid_codes[:].bitcast(FP8X4), scales=hid_scales[:], in_=hid[:].rearrange("p r t -> p (r t)")
+            )
+            bank = psum.tile([P, 2, width], F32, name="gate_bank")
+            for b in range(2):
+                nc.tensor.matmul_mx(
+                    out=bank[:, b, :],
+                    lhsT=w3_codes[:, P * b : P * (b + 1)].bitcast(FP8X4),
+                    lhsT_scale=w3_scales[:, P * b : P * (b + 1)],
+                    rhs=hid_codes[:].bitcast(FP8X4),
+                    rhs_scale=hid_scales[:],
+                    start=True,
+                    stop=True,
+                )
+            result = keep.tile([P, 2, width], F32, name="result%d" % chunk)
+            copy = nc.vector.tensor_copy if r1 == U else nc.scalar.copy
+            copy(out=result[:], in_=bank[:])
+            nc.sync.dma_start(out=out[:, r0:r1].rearrange("(b m) r -> m b r", b=2), in_=result[:])
+
+        sum_banks = [psum.tile([P, 2, 2, P], F32, name="sum_bank%d" % t, bufs=1) for t in range(PACK)]
+
+        def gate_path(t):
+            for h in range(2):
+                make_weights(t, h)
+                sum_members(sum_banks[t][:, 0], weight[t, h], h)
+
+        def value_path(t):
+            for h in range(2):
+                weigh_values(t, h)
+                sum_members(sum_banks[t][:, 1], weighted[t, h], h)
+
+        gather_scales(0)
+        gather_scales(1)
+        gather_words(0)
+        round_part(nc.scalar.copy, "w2", 0, 0, 64)
+        round_part(nc.scalar.copy, "w2", 1, 0, 24)
+        round_part(nc.vector.tensor_copy, "w2", 1, 24, 64)
+        quantize_tiles("w2", 0, 1)
+        gather_words(1)
+        quantize_tiles("w2", 1, 4)
+        round_part(nc.vector.tensor_copy, "w1", 0, 0, 64)
+        round_part(nc.vector.tensor_copy, "w1", 1, 0, 64)
+        quantize_tiles("w1", 0, 1)
+        quantize_tiles("w1", 1, 4)
+        split_unit()
+        for t in range(PACK):
+            gate_path(t)
+            pair_up(t, sum_banks[t][:, 0])
+        for t in range(PACK):
+            value_path(t)
+            invert(t, sum_banks[t][:, 0])
+            make_table(t, sum_banks[t][:, 1])
+        quantize_w3()
+        scale_loc()
+        for t, chunk in ((0, 0), (0, 1), (2, 0), (2, 1), (1, 0), (3, 0), (3, 1), (1, 1)):
+            look_up(t, chunk)
+        for chunk in range(3):
+            finish(chunk)

@@ -19,11 +19,12 @@ ACT = mybir.ActivationFunctionType
 P = 128
 PACK = 4
 SPARE = 16
+LEVELS = 3
+W2_ON_SCALAR = 24
+W1_ON_SCALAR = 0
 READER_CHUNKS = ((0, 256), (256, 512))
-SCALAR_BOTH = (0, 1)
-POOL_ADDS = (0, 1)
+SCALAR_BOTH = ((0, 0), (1, 0), (0, 1))
 FINISH_CHUNKS = ((0, 256), (256, 384), (384, 512))
-
 
 def tile_picked_ygistk_max_p_kernel(
     tc, x_words, x_scales, w1, w2, loc, unit, w3, offs, gt, gs, out
@@ -49,7 +50,7 @@ def tile_picked_ygistk_max_p_kernel(
         ident = keep.tile([P, P], F32, name="ident")
         tables = [keep.tile([P, V + SPARE], F32, name="table%d" % t) for t in range(PACK)]
 
-        nc.vector.memset(scale_win[:].bitcast(I32), 0)
+        nc.gpsimd.memset(scale_win[:].bitcast(I32), 0)
         nc.sync.dma_start(offs_t[:], offs)
         nc.sync.dma_start(out=unit_t[:], in_=unit.rearrange("(p j) o -> p (j o)", j=PACK))
         for q in range(4):
@@ -67,6 +68,7 @@ def tile_picked_ygistk_max_p_kernel(
         load_half("w2", w2, 1)
         load_half("w1", w1, 0)
         load_half("w1", w1, 1)
+
         nc.sync.dma_start(out=w3_raw[:], in_=w3.rearrange("(p j) m -> p j m", j=PACK))
         nc.sync.dma_start(gs_t[:], gs)
         nc.sync.dma_start(gt_t[:], gt)
@@ -91,7 +93,7 @@ def tile_picked_ygistk_max_p_kernel(
                 in_=word_win[:].bitcast(U32).indirect(offs_t[:, 32 * h : 32 * (h + 1)]),
             )
 
-        rounded, codes, scales = {}, {}, {}
+        rounded, codes = {}, {}
         for name in ("w2", "w1"):
             rounded[name] = keep.tile([P, PACK, P, PACK], BF16, name="rounded_" + name, align_bytes=64)
 
@@ -110,18 +112,18 @@ def tile_picked_ygistk_max_p_kernel(
                 in_=rounded[name][:, t0:t1, :, :].rearrange("p t m j -> p (t m j)"),
             )
             for t in range(t0, t1):
-                codes[name, t] = code[:, t - t0, :]
-                scales[name, t] = scale[:, t - t0, :]
+                codes[name, t] = (code[:, t - t0, :], scale[:, t - t0, :])
 
         def product(name, t, h, tag):
+            code, scale = codes[name, t]
             bank = psum.tile([P, D, P], F32, name=tag)
             for d in range(D):
                 nc.tensor.matmul_mx(
                     out=bank[:, d, :],
                     lhsT=x_w[h][:, d, :].bitcast(FP8X4),
                     lhsT_scale=x_sc[h][:, d, :],
-                    rhs=codes[name, t].bitcast(FP8X4),
-                    rhs_scale=scales[name, t],
+                    rhs=code.bitcast(FP8X4),
+                    rhs_scale=scale,
                     start=True,
                     stop=True,
                 )
@@ -141,21 +143,24 @@ def tile_picked_ygistk_max_p_kernel(
             weighted[t, h] = keep.tile([P, D, P], F32, name="weighted%d%d" % (t, h))
             nc.vector.tensor_tensor(weighted[t, h][:], bank[:], weight[t, h][:], ALU.mult)
 
-        def sum_members(bank, terms, h):
-            for d in range(D):
-                nc.tensor.matmul(
-                    out=bank[:, h, :],
-                    lhsT=terms[:, d, :],
-                    rhs=ident[:],
-                    is_transpose=True,
-                    start=(d == 0),
-                    stop=(d == D - 1),
-                )
+        def sum_members(terms, group, tag):
+            sums = psum.tile([P, len(group) * V], F32, name=tag)
+            for tt, t in enumerate(group):
+                for h in range(2):
+                    for d in range(D):
+                        nc.tensor.matmul(
+                            out=sums[:, V * tt + P * h : V * tt + P * (h + 1)],
+                            lhsT=terms[t, h][:, d, :],
+                            rhs=ident[:],
+                            is_transpose=True,
+                            start=(d == 0),
+                            stop=(d == D - 1),
+                        )
+            return sums
 
         sign = keep.tile([P, PACK], F32, name="sign")
         size = keep.tile([P, PACK], F32, name="size")
         loc_s = keep.tile([P, PACK, U], F32, name="loc_s")
-        w3_signed = keep.tile([P, PACK, N], F32, name="w3_signed")
         w3_rounded = keep.tile([P, N, PACK], BF16, name="w3_rounded", align_bytes=64)
         w3_codes = keep.tile([P, N], U32, name="w3_codes", align_bytes=64)
         w3_scales = keep.tile([P, N], U8, name="w3_scales", align_bytes=64)
@@ -166,71 +171,78 @@ def tile_picked_ygistk_max_p_kernel(
             nc.gpsimd.tensor_scalar(sign[:], step[:], 1.0, -1.0, ALU.mult, ALU.add)
             nc.gpsimd.tensor_tensor(size[:], unit_t[:], sign[:], ALU.mult)
 
-        def scale_loc():
+        def scale_loc(r0, r1):
             for t in range(PACK):
-                nc.gpsimd.tensor_scalar(loc_s[:, t, :], loc_t[:, t, :], size[:, t : t + 1], 0.0, ALU.mult, ALU.add)
+                nc.scalar.activation(loc_s[:, t, r0:r1], loc_t[:, t, r0:r1], ACT.Copy, scale=size[:, t : t + 1])
 
         def quantize_w3():
-            for j in range(PACK):
-                nc.gpsimd.tensor_scalar(w3_signed[:, j, :], w3_raw[:, j, :], sign[:, j : j + 1], 0.0, ALU.mult, ALU.add)
-            nc.gpsimd.tensor_copy(
-                out=w3_rounded[:].rearrange("p (c i) j -> p c j i", i=4),
-                in_=w3_signed[:].rearrange("p j (c i) -> p c j i", i=4),
+            nc.vector.tensor_tensor(
+                w3_rounded[:].rearrange("p (c i) j -> p c j i", i=4),
+                w3_raw[:].rearrange("p j (c i) -> p c j i", i=4),
+                sign[:].rearrange("p (c j i) -> p c j i", c=1, i=1).to_broadcast([P, N // 4, PACK, 4]),
+                ALU.mult,
             )
             nc.vector.quantize_mx(
                 out=w3_codes[:].bitcast(FP8X4), scales=w3_scales[:], in_=w3_rounded[:].rearrange("p m j -> p (m j)")
             )
 
-        inverse = {}
+        def invert(den, group, batch, depth):
+            parts = [group[0]] if batch else list(group)
+            width = len(group) * V // len(parts)
+            levels = {t: [den[:, width * n : width * (n + 1)]] for n, t in enumerate(parts)}
+            for level in range(depth):
+                width //= 2
+                for t in parts:
+                    below = levels[t][-1]
+                    joined = keep.tile([P, width], F32, name="joined%d_%d" % (t, level))
+                    if level == 0:
+                        nc.vector.tensor_reduce(
+                            joined[:], below.rearrange("p (a v) -> p v a", a=2), mybir.AxisListType.X, ALU.mult
+                        )
+                    else:
+                        nc.vector.tensor_tensor(joined[:], below[:, :width], below[:, width:], ALU.mult)
+                    levels[t].append(joined[:])
+            inverse = {}
+            for t in parts:
+                inverse[t] = keep.tile([P, 1, width], F32, name="inverse%d_top" % t)
+                nc.vector.reciprocal(inverse[t][:, 0, :], levels[t][depth])
+            for level in range(depth):
+                for t in parts:
+                    wider = keep.tile([P, 1, 2 * width], F32, name="wider", tag="inverse%d_%d" % (t, 2 * width))
+                    nc.vector.tensor_tensor(
+                        wider[:, 0, :].rearrange("p (a v) -> p a v", a=2),
+                        levels[t][depth - 1 - level].rearrange("p (a v) -> p a v", a=2)[:, ::-1, :],
+                        inverse[t][:].to_broadcast([P, 2, width]),
+                        ALU.mult,
+                    )
+                    inverse[t] = wider
+                width *= 2
+            if batch:
+                return {t: inverse[group[0]][:, 0, V * n : V * (n + 1)] for n, t in enumerate(group)}
+            return {t: inverse[t][:, 0, :] for t in group}
 
-        pairs = {}
+        def make_tables(group, num, inverse):
+            for tt, t in enumerate(group):
+                nc.vector.scalar_tensor_tensor(
+                    tables[t][:, :V], num[:, V * tt : V * (tt + 1)], size[:, t : t + 1], inverse[t], ALU.mult, ALU.mult
+                )
 
-        def pair_up(t, den_bank):
-            two = keep.tile([P, 2, P // 2], F32, name="two%d" % t)
-            nc.vector.tensor_reduce(
-                two[:].rearrange("p a v -> p (a v)"), den_bank.rearrange("p h v -> p v h"), mybir.AxisListType.X, ALU.mult
-            )
-            four = ring.tile([P, P // 2], F32, name="four")
-            nc.vector.tensor_reduce(four[:], two[:].rearrange("p a v -> p v a"), mybir.AxisListType.X, ALU.mult)
-            inv_four = ring.tile([P, 1, P // 2], F32, name="inv_four")
-            nc.vector.reciprocal(inv_four[:, 0, :], four[:])
-            inv_two = keep.tile([P, 1, P], F32, name="inv_two%d" % t)
-            nc.gpsimd.tensor_tensor(
-                inv_two[:, 0, :].rearrange("p (a v) -> p a v", a=2),
-                two[:, ::-1, :],
-                inv_four[:].to_broadcast([P, 2, P // 2]),
-                ALU.mult,
-            )
-            pairs[t] = inv_two
+        fetched = {}
 
-        def invert(t, den_bank):
-            inv_two = pairs[t]
-            inverse[t] = keep.tile([P, 2, P], F32, name="inverse%d" % t)
-            nc.vector.tensor_tensor(inverse[t][:], den_bank[:, ::-1, :], inv_two[:].to_broadcast([P, 2, P]), ALU.mult)
-
-        def make_table(t, num_bank):
-            nc.vector.scalar_tensor_tensor(
-                tables[t][:, :V],
-                num_bank.rearrange("p h v -> p (h v)"),
-                size[:, t : t + 1],
-                inverse[t][:].rearrange("p h v -> p (h v)"),
-                ALU.mult,
-                ALU.mult,
-            )
-
-        diff = [keep.tile([P, PACK, r1 - r0], F32, name="diff%d" % r0) for r0, r1 in READER_CHUNKS]
-
-        def look_up(t, chunk):
+        def fetch(t, chunk):
             r0, r1 = READER_CHUNKS[chunk]
             other = keep.tile([P, r1 - r0], F32, name="other%d_%d" % (t, chunk))
             nc.scalar.activation(other[:], tables[t][:].indirect(gs_t[:, r0 // 16 : r1 // 16]), ACT.Copy, scale=-0.6)
             own = tables[t][:].indirect(gt_t[:, r0 // 16 : r1 // 16])
-            if t in SCALAR_BOTH:
-                fetched = keep.tile([P, r1 - r0], F32, name="fetched%d_%d" % (t, chunk))
-                nc.scalar.activation(fetched[:], own, ACT.Copy)
-                own = fetched[:]
-            adder = nc.gpsimd if t in POOL_ADDS else nc.vector
-            adder.tensor_tensor(diff[chunk][:, t, :], own, other[:], ALU.add)
+            if (t, chunk) in SCALAR_BOTH:
+                copied = keep.tile([P, r1 - r0], F32, name="own%d_%d" % (t, chunk))
+                nc.scalar.activation(copied[:], own, ACT.Copy)
+                own = copied[:]
+            fetched[t, chunk] = (own, other)
+
+        def subtract(t, chunk):
+            own, other = fetched[t, chunk]
+            nc.vector.tensor_tensor(diff[:, chunk, t, :], own, other[:], ALU.add)
 
         def finish(chunk):
             r0, r1 = FINISH_CHUNKS[chunk]
@@ -239,7 +251,7 @@ def tile_picked_ygistk_max_p_kernel(
             hid = keep.tile([P, width, PACK], BF16, name="hid%d" % chunk, align_bytes=64)
             nc.vector.tensor_tensor(
                 hid[:].rearrange("p (c i) t -> p c t i", i=4),
-                diff[half][:, :, c0 : c0 + width].rearrange("p t (c i) -> p c t i", i=4),
+                diff[:, half, :, c0 : c0 + width].rearrange("p t (c i) -> p c t i", i=4),
                 loc_s[:, :, r0:r1].rearrange("p t (c i) -> p c t i", i=4),
                 ALU.max,
             )
@@ -260,46 +272,50 @@ def tile_picked_ygistk_max_p_kernel(
                     stop=True,
                 )
             result = keep.tile([P, 2, width], F32, name="result%d" % chunk)
-            copy = nc.vector.tensor_copy if r1 == U else nc.scalar.copy
-            copy(out=result[:], in_=bank[:])
+            nc.scalar.copy(out=result[:], in_=bank[:])
             nc.sync.dma_start(out=out[:, r0:r1].rearrange("(b m) r -> m b r", b=2), in_=result[:])
-
-        sum_banks = [psum.tile([P, 2, 2, P], F32, name="sum_bank%d" % t, bufs=1) for t in range(PACK)]
-
-        def gate_path(t):
-            for h in range(2):
-                make_weights(t, h)
-                sum_members(sum_banks[t][:, 0], weight[t, h], h)
-
-        def value_path(t):
-            for h in range(2):
-                weigh_values(t, h)
-                sum_members(sum_banks[t][:, 1], weighted[t, h], h)
 
         gather_scales(0)
         gather_scales(1)
         gather_words(0)
-        round_part(nc.scalar.copy, "w2", 0, 0, 64)
-        round_part(nc.scalar.copy, "w2", 1, 0, 24)
-        round_part(nc.vector.tensor_copy, "w2", 1, 24, 64)
-        quantize_tiles("w2", 0, 1)
         gather_words(1)
-        quantize_tiles("w2", 1, 4)
-        round_part(nc.vector.tensor_copy, "w1", 0, 0, 64)
+        round_part(nc.scalar.copy, "w2", 0, 0, 64)
+        round_part(nc.scalar.copy, "w2", 1, 0, W2_ON_SCALAR)
+        round_part(nc.vector.tensor_copy, "w2", 1, W2_ON_SCALAR, 64)
+        for t0, t1 in ((0, 1), (1, 4)):
+            quantize_tiles("w2", t0, t1)
+
+        round_part(nc.vector.tensor_copy, "w1", 0, W1_ON_SCALAR, 64)
         round_part(nc.vector.tensor_copy, "w1", 1, 0, 64)
-        quantize_tiles("w1", 0, 1)
-        quantize_tiles("w1", 1, 4)
+        for t0, t1 in ((0, 1), (1, 4)):
+            quantize_tiles("w1", t0, t1)
         split_unit()
         for t in range(PACK):
-            gate_path(t)
-            pair_up(t, sum_banks[t][:, 0])
-        for t in range(PACK):
-            value_path(t)
-            invert(t, sum_banks[t][:, 0])
-            make_table(t, sum_banks[t][:, 1])
+            for h in range(2):
+                make_weights(t, h)
+                weigh_values(t, h)
+        groups = (((0,), True, 2), ((1,), True, 2), ((2, 3), False, 2))
+        inverses = [invert(sum_members(weight, groups[0][0], "den_bank")[:], *groups[0])]
+        for g, (group, batch, depth) in enumerate(groups):
+            for following in groups[g + 1 : g + 2]:
+                inverses.append(invert(sum_members(weight, following[0], "den_bank")[:], *following))
+            make_tables(group, sum_members(weighted, group, "num_bank"), inverses[g])
         quantize_w3()
-        scale_loc()
-        for t, chunk in ((0, 0), (0, 1), (2, 0), (2, 1), (1, 0), (3, 0), (3, 1), (1, 1)):
-            look_up(t, chunk)
-        for chunk in range(3):
-            finish(chunk)
+        for r0, r1 in READER_CHUNKS:
+            scale_loc(r0, r1)
+        for chunk in range(2):
+            for t in range(2):
+                fetch(t, chunk)
+        for chunk in range(2):
+            for t in range(2, 4):
+                fetch(t, chunk)
+        diff = keep.tile([P, 2, PACK, U // 2], F32, name="diff", tag="inverse2_256")
+        for chunk in range(2):
+            for t in range(2):
+                subtract(t, chunk)
+        for chunk in range(2):
+            for t in range(2, 4):
+                subtract(t, chunk)
+            for part in range(len(FINISH_CHUNKS)):
+                if FINISH_CHUNKS[part][0] // 256 == chunk:
+                    finish(part)

@@ -20,10 +20,11 @@ P = 128
 PACK = 4
 SPARE = 16
 LEVELS = 3
-W2_ON_SCALAR = 24
+W2_ON_SCALAR = 44
 W1_ON_SCALAR = 0
+BANKS = {"gate_bank": 2, "value_bank": 2, "den_bank": 2, "num_bank": 2}
 READER_CHUNKS = ((0, 256), (256, 512))
-SCALAR_BOTH = ((0, 0), (1, 0), (0, 1))
+SCALAR_BOTH = ((0, 0), (0, 1), (2, 1), (3, 1))
 FINISH_CHUNKS = ((0, 256), (256, 384), (384, 512))
 
 def tile_picked_ygistk_max_p_kernel(
@@ -42,8 +43,7 @@ def tile_picked_ygistk_max_p_kernel(
         word_win = keep.tile([P, T], I32, name="word_win", align_bytes=64)
         raw = {}
         for name in ("w2", "w1"):
-            for c in range(2):
-                raw[name, c] = keep.tile([P, PACK, H // 2], F32, name="raw_%s_%d" % (name, c))
+            raw[name] = keep.tile([P, PACK, H], F32, name="raw_" + name)
         unit_t = keep.tile([P, PACK], F32, name="unit_t")
         loc_t = keep.tile([P, PACK, U], F32, name="loc_t")
         w3_raw = keep.tile([P, PACK, N], F32, name="w3_raw")
@@ -59,17 +59,11 @@ def tile_picked_ygistk_max_p_kernel(
                 in_=x_scales[0, 4 * q : 4 * q + 4, :].bitcast(I32),
             )
 
-        def load_half(name, w, c):
-            cols = w[:, c * (H // 2) : (c + 1) * (H // 2)]
-            nc.sync.dma_start(out=raw[name, c][:], in_=cols.rearrange("(p j) c -> p j c", j=PACK))
-
         nc.sync.dma_start(out=word_win[:], in_=x_words[0].rearrange("p n t -> p (n t)").bitcast(I32))
-        load_half("w2", w2, 0)
-        load_half("w2", w2, 1)
-        load_half("w1", w1, 0)
-        load_half("w1", w1, 1)
-
+        nc.sync.dma_start(out=raw["w2"][:], in_=w2.rearrange("(p j) c -> p j c", j=PACK))
         nc.sync.dma_start(out=w3_raw[:], in_=w3.rearrange("(p j) m -> p j m", j=PACK))
+        nc.sync.dma_start(out=raw["w1"][:], in_=w1.rearrange("(p j) c -> p j c", j=PACK))
+
         nc.sync.dma_start(gs_t[:], gs)
         nc.sync.dma_start(gt_t[:], gt)
         nc.sync.dma_start(out=loc_t[:], in_=loc.rearrange("(p j) r -> p j r", j=PACK))
@@ -94,13 +88,11 @@ def tile_picked_ygistk_max_p_kernel(
             )
 
         rounded, codes = {}, {}
-        for name in ("w2", "w1"):
-            rounded[name] = keep.tile([P, PACK, P, PACK], BF16, name="rounded_" + name, align_bytes=64)
 
-        def round_part(copy, name, c, m0, m1):
+        def round_part(copy, name, m0, m1):
             copy(
-                out=rounded[name][:, :, 64 * c + m0 : 64 * c + m1, :].rearrange("p t m j -> p m j t"),
-                in_=raw[name, c][:, :, PACK * m0 : PACK * m1].rearrange("p j (m t) -> p m j t", t=PACK),
+                out=rounded[name][:, :, m0:m1, :].rearrange("p t m j -> p m j t"),
+                in_=raw[name][:, :, PACK * m0 : PACK * m1].rearrange("p j (m t) -> p m j t", t=PACK),
             )
 
         def quantize_tiles(name, t0, t1):
@@ -116,7 +108,7 @@ def tile_picked_ygistk_max_p_kernel(
 
         def product(name, t, h, tag):
             code, scale = codes[name, t]
-            bank = psum.tile([P, D, P], F32, name=tag)
+            bank = psum.tile([P, D, P], F32, name=tag, bufs=BANKS[tag])
             for d in range(D):
                 nc.tensor.matmul_mx(
                     out=bank[:, d, :],
@@ -144,7 +136,7 @@ def tile_picked_ygistk_max_p_kernel(
             nc.vector.tensor_tensor(weighted[t, h][:], bank[:], weight[t, h][:], ALU.mult)
 
         def sum_members(terms, group, tag):
-            sums = psum.tile([P, len(group) * V], F32, name=tag)
+            sums = psum.tile([P, len(group) * V], F32, name=tag, bufs=BANKS[tag])
             for tt, t in enumerate(group):
                 for h in range(2):
                     for d in range(D):
@@ -161,7 +153,6 @@ def tile_picked_ygistk_max_p_kernel(
         sign = keep.tile([P, PACK], F32, name="sign")
         size = keep.tile([P, PACK], F32, name="size")
         loc_s = keep.tile([P, PACK, U], F32, name="loc_s")
-        w3_rounded = keep.tile([P, N, PACK], BF16, name="w3_rounded", align_bytes=64)
         w3_codes = keep.tile([P, N], U32, name="w3_codes", align_bytes=64)
         w3_scales = keep.tile([P, N], U8, name="w3_scales", align_bytes=64)
 
@@ -176,6 +167,7 @@ def tile_picked_ygistk_max_p_kernel(
                 nc.scalar.activation(loc_s[:, t, r0:r1], loc_t[:, t, r0:r1], ACT.Copy, scale=size[:, t : t + 1])
 
         def quantize_w3():
+            w3_rounded = keep.tile([P, N, PACK], BF16, name="rounded", align_bytes=64)
             nc.vector.tensor_tensor(
                 w3_rounded[:].rearrange("p (c i) j -> p c j i", i=4),
                 w3_raw[:].rearrange("p j (c i) -> p c j i", i=4),
@@ -260,7 +252,8 @@ def tile_picked_ygistk_max_p_kernel(
             nc.vector.quantize_mx(
                 out=hid_codes[:].bitcast(FP8X4), scales=hid_scales[:], in_=hid[:].rearrange("p r t -> p (r t)")
             )
-            bank = psum.tile([P, 2, width], F32, name="gate_bank")
+            tag = ("gate_bank", "value_bank")[chunk % 2]
+            bank = psum.tile([P, 2, width], F32, name=tag, bufs=BANKS[tag])
             for b in range(2):
                 nc.tensor.matmul_mx(
                     out=bank[:, b, :],
@@ -272,35 +265,39 @@ def tile_picked_ygistk_max_p_kernel(
                     stop=True,
                 )
             result = keep.tile([P, 2, width], F32, name="result%d" % chunk)
-            nc.scalar.copy(out=result[:], in_=bank[:])
+            copy = nc.vector.tensor_copy if r1 == U else nc.scalar.copy
+            copy(out=result[:], in_=bank[:])
             nc.sync.dma_start(out=out[:, r0:r1].rearrange("(b m) r -> m b r", b=2), in_=result[:])
 
         gather_scales(0)
         gather_scales(1)
         gather_words(0)
         gather_words(1)
-        round_part(nc.scalar.copy, "w2", 0, 0, 64)
-        round_part(nc.scalar.copy, "w2", 1, 0, W2_ON_SCALAR)
-        round_part(nc.vector.tensor_copy, "w2", 1, W2_ON_SCALAR, 64)
+        rounded["w2"] = keep.tile([P, PACK, P, PACK], BF16, name="rounded", align_bytes=64)
+        round_part(nc.scalar.copy, "w2", 0, W2_ON_SCALAR)
+        round_part(nc.vector.tensor_copy, "w2", W2_ON_SCALAR, P)
         for t0, t1 in ((0, 1), (1, 4)):
             quantize_tiles("w2", t0, t1)
 
-        round_part(nc.vector.tensor_copy, "w1", 0, W1_ON_SCALAR, 64)
-        round_part(nc.vector.tensor_copy, "w1", 1, 0, 64)
+        split_unit()
+        quantize_w3()
+        rounded["w1"] = keep.tile([P, PACK, P, PACK], BF16, name="rounded", align_bytes=64)
+        round_part(nc.vector.tensor_copy, "w1", 0, P)
         for t0, t1 in ((0, 1), (1, 4)):
             quantize_tiles("w1", t0, t1)
-        split_unit()
-        for t in range(PACK):
-            for h in range(2):
-                make_weights(t, h)
-                weigh_values(t, h)
-        groups = (((0,), True, 2), ((1,), True, 2), ((2, 3), False, 2))
-        inverses = [invert(sum_members(weight, groups[0][0], "den_bank")[:], *groups[0])]
-        for g, (group, batch, depth) in enumerate(groups):
-            for following in groups[g + 1 : g + 2]:
-                inverses.append(invert(sum_members(weight, following[0], "den_bank")[:], *following))
-            make_tables(group, sum_members(weighted, group, "num_bank"), inverses[g])
-        quantize_w3()
+        inverse = {}
+        groups = {0: [(0,)], 1: [(1,)], 3: [(2, 3)]}
+        for s in range(PACK + 2):
+            if s < PACK:
+                for h in range(2):
+                    make_weights(s, h)
+            if 0 <= s - 1 < PACK:
+                inverse.update(invert(sum_members(weight, (s - 1,), "den_bank")[:], (s - 1,), False, 2))
+            if 0 <= s - 1 < PACK:
+                for h in range(2):
+                    weigh_values(s - 1, h)
+            if 0 <= s - 2 < PACK:
+                make_tables((s - 2,), sum_members(weighted, (s - 2,), "num_bank"), inverse)
         for r0, r1 in READER_CHUNKS:
             scale_loc(r0, r1)
         for chunk in range(2):

@@ -20,11 +20,11 @@ P = 128
 PACK = 4
 SPARE = 16
 LEVELS = 3
-W2_ON_SCALAR = 44
+W2_ON_SCALAR = 16
 W1_ON_SCALAR = 0
 BANKS = {"gate_bank": 2, "value_bank": 2, "den_bank": 2, "num_bank": 2}
 READER_CHUNKS = ((0, 256), (256, 512))
-SCALAR_BOTH = ((0, 0), (0, 1), (2, 1), (3, 1))
+SCALAR_BOTH = ((0, 0), (0, 1), (1, 0), (1, 1), (3, 1))
 FINISH_CHUNKS = ((0, 256), (256, 384), (384, 512))
 
 def tile_picked_ygistk_max_p_kernel(
@@ -43,7 +43,8 @@ def tile_picked_ygistk_max_p_kernel(
         word_win = keep.tile([P, T], I32, name="word_win", align_bytes=64)
         raw = {}
         for name in ("w2", "w1"):
-            raw[name] = keep.tile([P, PACK, H], F32, name="raw_" + name)
+            for c in range(2):
+                raw[name, c] = keep.tile([P, PACK, H // 2], F32, name="raw_%s_%d" % (name, c), align_bytes=64)
         unit_t = keep.tile([P, PACK], F32, name="unit_t")
         loc_t = keep.tile([P, PACK, U], F32, name="loc_t")
         w3_raw = keep.tile([P, PACK, N], F32, name="w3_raw")
@@ -59,10 +60,16 @@ def tile_picked_ygistk_max_p_kernel(
                 in_=x_scales[0, 4 * q : 4 * q + 4, :].bitcast(I32),
             )
 
+        def load_half(name, w, c):
+            cols = w[:, c * (H // 2) : (c + 1) * (H // 2)]
+            nc.sync.dma_start(out=raw[name, c][:], in_=cols.rearrange("(p j) c -> p j c", j=PACK))
+
         nc.sync.dma_start(out=word_win[:], in_=x_words[0].rearrange("p n t -> p (n t)").bitcast(I32))
-        nc.sync.dma_start(out=raw["w2"][:], in_=w2.rearrange("(p j) c -> p j c", j=PACK))
+        load_half("w2", w2, 0)
+        load_half("w2", w2, 1)
         nc.sync.dma_start(out=w3_raw[:], in_=w3.rearrange("(p j) m -> p j m", j=PACK))
-        nc.sync.dma_start(out=raw["w1"][:], in_=w1.rearrange("(p j) c -> p j c", j=PACK))
+        load_half("w1", w1, 0)
+        load_half("w1", w1, 1)
 
         nc.sync.dma_start(gs_t[:], gs)
         nc.sync.dma_start(gt_t[:], gt)
@@ -89,10 +96,10 @@ def tile_picked_ygistk_max_p_kernel(
 
         rounded, codes = {}, {}
 
-        def round_part(copy, name, m0, m1):
+        def round_part(copy, name, c, m0, m1):
             copy(
-                out=rounded[name][:, :, m0:m1, :].rearrange("p t m j -> p m j t"),
-                in_=raw[name][:, :, PACK * m0 : PACK * m1].rearrange("p j (m t) -> p m j t", t=PACK),
+                out=rounded[name][:, :, 64 * c + m0 : 64 * c + m1, :].rearrange("p t m j -> p m j t"),
+                in_=raw[name, c][:, :, PACK * m0 : PACK * m1].rearrange("p j (m t) -> p m j t", t=PACK),
             )
 
         def quantize_tiles(name, t0, t1):
@@ -153,7 +160,6 @@ def tile_picked_ygistk_max_p_kernel(
         sign = keep.tile([P, PACK], F32, name="sign")
         size = keep.tile([P, PACK], F32, name="size")
         loc_s = keep.tile([P, PACK, U], F32, name="loc_s")
-        w3_codes = keep.tile([P, N], U32, name="w3_codes", align_bytes=64)
         w3_scales = keep.tile([P, N], U8, name="w3_scales", align_bytes=64)
 
         def split_unit():
@@ -164,16 +170,19 @@ def tile_picked_ygistk_max_p_kernel(
 
         def scale_loc(r0, r1):
             for t in range(PACK):
-                nc.scalar.activation(loc_s[:, t, r0:r1], loc_t[:, t, r0:r1], ACT.Copy, scale=size[:, t : t + 1])
+                nc.gpsimd.tensor_scalar(loc_s[:, t, r0:r1], loc_t[:, t, r0:r1], size[:, t : t + 1], 0.0, ALU.mult, ALU.add)
 
         def quantize_w3():
-            w3_rounded = keep.tile([P, N, PACK], BF16, name="rounded", align_bytes=64)
+            w3_rounded = keep.tile([P, N, PACK], BF16, name="w3_rounded", tag="raw_w2_1", align_bytes=64)
             nc.vector.tensor_tensor(
                 w3_rounded[:].rearrange("p (c i) j -> p c j i", i=4),
                 w3_raw[:].rearrange("p j (c i) -> p c j i", i=4),
                 sign[:].rearrange("p (c j i) -> p c j i", c=1, i=1).to_broadcast([P, N // 4, PACK, 4]),
                 ALU.mult,
             )
+            return w3_rounded
+
+        def pack_w3(w3_rounded):
             nc.vector.quantize_mx(
                 out=w3_codes[:].bitcast(FP8X4), scales=w3_scales[:], in_=w3_rounded[:].rearrange("p m j -> p (m j)")
             )
@@ -187,7 +196,7 @@ def tile_picked_ygistk_max_p_kernel(
                 for t in parts:
                     below = levels[t][-1]
                     joined = keep.tile([P, width], F32, name="joined%d_%d" % (t, level))
-                    if level == 0:
+                    if level == 0 or True:
                         nc.vector.tensor_reduce(
                             joined[:], below.rearrange("p (a v) -> p v a", a=2), mybir.AxisListType.X, ALU.mult
                         )
@@ -274,17 +283,21 @@ def tile_picked_ygistk_max_p_kernel(
         gather_words(0)
         gather_words(1)
         rounded["w2"] = keep.tile([P, PACK, P, PACK], BF16, name="rounded", align_bytes=64)
-        round_part(nc.scalar.copy, "w2", 0, W2_ON_SCALAR)
-        round_part(nc.vector.tensor_copy, "w2", W2_ON_SCALAR, P)
+        round_part(nc.scalar.copy, "w2", 0, 0, 64)
+        round_part(nc.scalar.copy, "w2", 1, 0, W2_ON_SCALAR)
+        round_part(nc.vector.tensor_copy, "w2", 1, W2_ON_SCALAR, 64)
         for t0, t1 in ((0, 1), (1, 4)):
             quantize_tiles("w2", t0, t1)
 
         split_unit()
-        quantize_w3()
-        rounded["w1"] = keep.tile([P, PACK, P, PACK], BF16, name="rounded", align_bytes=64)
-        round_part(nc.vector.tensor_copy, "w1", 0, P)
+        w3_ready = quantize_w3()
+        rounded["w1"] = keep.tile([P, PACK, P, PACK], BF16, name="rounded_w1", align_bytes=64)
+        round_part(nc.vector.tensor_copy, "w1", 0, W1_ON_SCALAR, 64)
+        round_part(nc.vector.tensor_copy, "w1", 1, 0, 64)
         for t0, t1 in ((0, 1), (1, 4)):
             quantize_tiles("w1", t0, t1)
+        w3_codes = keep.tile([P, N], U32, name="w3_codes", tag="raw_w1_1", align_bytes=64)
+        pack_w3(w3_ready)
         inverse = {}
         groups = {0: [(0,)], 1: [(1,)], 3: [(2, 3)]}
         for s in range(PACK + 2):

from contextlib import ExitStack

import concourse.mybir as mybir
from concourse.masks import make_identity

K, T, S, D, N, H, V, U = 512, 2048, 1024, 4, 256, 512, 256, 512
FLOPS = 2 * K * H * S * 2 + 2 * H * N * U

F32 = mybir.dt.float32
BF16 = mybir.dt.bfloat16
I32 = mybir.dt.int32
U32 = mybir.dt.uint32
U16 = mybir.dt.uint16
U8 = mybir.dt.uint8
FP8X4 = mybir.dt.float8_e4m3fn_x4
ALU = mybir.AluOpType
ACT = mybir.ActivationFunctionType

P = 128
PACK = 4
SPARE = 16
LEVELS = 3
W2_ON_SCALAR = 16
W1_ON_SCALAR = 0
BANKS = {"gate_bank": 2, "value_bank": 2, "den_bank": 2, "num_bank": 2}
READER_CHUNKS = ((0, 256), (256, 512))
SCALAR_BOTH = ((0, 0), (0, 1), (1, 0), (1, 1), (3, 1))
FINISH_CHUNKS = ((0, 256), (256, 384), (384, 512))

def tile_picked_ygistk_max_p_kernel(
    tc, x_words, x_scales, w1, w2, loc, unit, w3, offs, gt, gs, out
):
    nc = tc.nc
    with ExitStack() as ctx:
        keep = ctx.enter_context(tc.tile_pool(name="keep", bufs=1))
        ring = ctx.enter_context(tc.tile_pool(name="ring", bufs=2))
        psum = ctx.enter_context(tc.psum_pool(name="psum", bufs=2))

        offs_t = keep.tile([P, S // 16], U16, name="offs_t")
        gt_t = keep.tile([P, U // 16], U16, name="gt_t")
        gs_t = keep.tile([P, U // 16], U16, name="gs_t")
        scale_win = keep.tile([P, T], U8, name="scale_win", align_bytes=64)
        word_win = keep.tile([P, T], I32, name="word_win", align_bytes=64)
        raw = {}
        for name in ("w2", "w1"):
            for c in range(2):
                raw[name, c] = keep.tile([P, PACK, H // 2], F32, name="raw_%s_%d" % (name, c), align_bytes=64)
        unit_t = keep.tile([P, PACK], F32, name="unit_t")
        loc_t = keep.tile([P, PACK, U], F32, name="loc_t")
        w3_raw = keep.tile([P, PACK, N], F32, name="w3_raw")
        ident = keep.tile([P, P], F32, name="ident")
        tables = [keep.tile([P, V + SPARE], F32, name="table%d" % t) for t in range(PACK)]

        nc.gpsimd.memset(scale_win[:].bitcast(I32), 0)
        nc.sync.dma_start(offs_t[:], offs)
        nc.sync.dma_start(out=unit_t[:], in_=unit.rearrange("(p j) o -> p (j o)", j=PACK))
        for q in range(4):
            nc.sync.dma_start(
                out=scale_win[32 * q : 32 * q + 4, :].bitcast(I32),
                in_=x_scales[0, 4 * q : 4 * q + 4, :].bitcast(I32),
            )

        def load_half(name, w, c):
            cols = w[:, c * (H // 2) : (c + 1) * (H // 2)]
            nc.sync.dma_start(out=raw[name, c][:], in_=cols.rearrange("(p j) c -> p j c", j=PACK))

        nc.sync.dma_start(out=word_win[:], in_=x_words[0].rearrange("p n t -> p (n t)").bitcast(I32))
        load_half("w2", w2, 0)
        load_half("w2", w2, 1)
        nc.sync.dma_start(out=w3_raw[:], in_=w3.rearrange("(p j) m -> p j m", j=PACK))
        load_half("w1", w1, 0)
        load_half("w1", w1, 1)

        nc.sync.dma_start(gs_t[:], gs)
        nc.sync.dma_start(gt_t[:], gt)
        nc.sync.dma_start(out=loc_t[:], in_=loc.rearrange("(p j) r -> p j r", j=PACK))

        make_identity(nc, ident[:])
        for t in range(PACK):
            nc.gpsimd.memset(tables[t][:, V:], 0.0)

        x_sc = [keep.tile([P, D, P], U8, name="x_sc%d" % h, align_bytes=64) for h in range(2)]
        x_w = [keep.tile([P, D, P], U32, name="x_w%d" % h, align_bytes=64) for h in range(2)]

        def gather_scales(h):
            nc.vector.tensor_copy(
                out=x_sc[h][:].rearrange("p d v -> p v d"),
                in_=scale_win[:].indirect(offs_t[:, 32 * h : 32 * (h + 1)]),
            )

        def gather_words(h):
            nc.vector.tensor_copy(
                out=x_w[h][:].rearrange("p d v -> p v d"),
                in_=word_win[:].bitcast(U32).indirect(offs_t[:, 32 * h : 32 * (h + 1)]),
            )

        rounded, codes = {}, {}

        def round_part(copy, name, c, m0, m1):
            copy(
                out=rounded[name][:, :, 64 * c + m0 : 64 * c + m1, :].rearrange("p t m j -> p m j t"),
                in_=raw[name, c][:, :, PACK * m0 : PACK * m1].rearrange("p j (m t) -> p m j t", t=PACK),
            )

        def quantize_tiles(name, t0, t1):
            code = keep.tile([P, t1 - t0, P], U32, name="codes_%s_%d" % (name, t0), align_bytes=64)
            scale = keep.tile([P, t1 - t0, P], U8, name="scales_%s_%d" % (name, t0), align_bytes=64)
            nc.vector.quantize_mx(
                out=code[:].rearrange("p t m -> p (t m)").bitcast(FP8X4),
                scales=scale[:].rearrange("p t m -> p (t m)"),
                in_=rounded[name][:, t0:t1, :, :].rearrange("p t m j -> p (t m j)"),
            )
            for t in range(t0, t1):
                codes[name, t] = (code[:, t - t0, :], scale[:, t - t0, :])

        def product(name, t, h, tag):
            code, scale = codes[name, t]
            bank = psum.tile([P, D, P], F32, name=tag, bufs=BANKS[tag])
            for d in range(D):
                nc.tensor.matmul_mx(
                    out=bank[:, d, :],
                    lhsT=x_w[h][:, d, :].bitcast(FP8X4),
                    lhsT_scale=x_sc[h][:, d, :],
                    rhs=code.bitcast(FP8X4),
                    rhs_scale=scale,
                    start=True,
                    stop=True,
                )
            return bank

        weight, weighted = {}, {}

        def make_weights(t, h):
            bank = product("w2", t, h, "gate_bank")
            squashed = ring.tile([P, D, P], F32, name="squashed")
            nc.scalar.activation(squashed[:], bank[:], ACT.Tanh)
            weight[t, h] = keep.tile([P, D, P], F32, name="weight%d%d" % (t, h))
            nc.scalar.activation(weight[t, h][:], squashed[:], ACT.Exp, scale=1.3)

        def weigh_values(t, h):
            bank = product("w1", t, h, "value_bank")
            weighted[t, h] = keep.tile([P, D, P], F32, name="weighted%d%d" % (t, h))
            nc.vector.tensor_tensor(weighted[t, h][:], bank[:], weight[t, h][:], ALU.mult)

        def sum_members(terms, group, tag):
            sums = psum.tile([P, len(group) * V], F32, name=tag, bufs=BANKS[tag])
            for tt, t in enumerate(group):
                for h in range(2):
                    for d in range(D):
                        nc.tensor.matmul(
                            out=sums[:, V * tt + P * h : V * tt + P * (h + 1)],
                            lhsT=terms[t, h][:, d, :],
                            rhs=ident[:],
                            is_transpose=True,
                            start=(d == 0),
                            stop=(d == D - 1),
                        )
            return sums

        sign = keep.tile([P, PACK], F32, name="sign")
        size = keep.tile([P, PACK], F32, name="size")
        loc_s = keep.tile([P, PACK, U], F32, name="loc_s")
        w3_scales = keep.tile([P, N], U8, name="w3_scales", align_bytes=64)

        def split_unit():
            step = keep.tile([P, PACK], F32, name="step")
            nc.gpsimd.tensor_scalar(step[:], unit_t[:], 0.0, 2.0, ALU.is_ge, ALU.mult)
            nc.gpsimd.tensor_scalar(sign[:], step[:], 1.0, -1.0, ALU.mult, ALU.add)
            nc.gpsimd.tensor_tensor(size[:], unit_t[:], sign[:], ALU.mult)

        def scale_loc(r0, r1):
            for t in range(PACK):
                nc.gpsimd.tensor_scalar(loc_s[:, t, r0:r1], loc_t[:, t, r0:r1], size[:, t : t + 1], 0.0, ALU.mult, ALU.add)

        def quantize_w3():
            w3_rounded = keep.tile([P, N, PACK], BF16, name="w3_rounded", tag="raw_w2_1", align_bytes=64)
            nc.vector.tensor_tensor(
                w3_rounded[:].rearrange("p (c i) j -> p c j i", i=4),
                w3_raw[:].rearrange("p j (c i) -> p c j i", i=4),
                sign[:].rearrange("p (c j i) -> p c j i", c=1, i=1).to_broadcast([P, N // 4, PACK, 4]),
                ALU.mult,
            )
            return w3_rounded

        def pack_w3(w3_rounded):
            nc.vector.quantize_mx(
                out=w3_codes[:].bitcast(FP8X4), scales=w3_scales[:], in_=w3_rounded[:].rearrange("p m j -> p (m j)")
            )

        def invert(den, group, batch, depth):
            parts = [group[0]] if batch else list(group)
            width = len(group) * V // len(parts)
            levels = {t: [den[:, width * n : width * (n + 1)]] for n, t in enumerate(parts)}
            for level in range(depth):
                width //= 2
                for t in parts:
                    below = levels[t][-1]
                    joined = keep.tile([P, width], F32, name="joined%d_%d" % (t, level))
                    if level == 0 or True:
                        nc.vector.tensor_reduce(
                            joined[:], below.rearrange("p (a v) -> p v a", a=2), mybir.AxisListType.X, ALU.mult
                        )
                    else:
                        nc.vector.tensor_tensor(joined[:], below[:, :width], below[:, width:], ALU.mult)
                    levels[t].append(joined[:])
            inverse = {}
            for t in parts:
                inverse[t] = keep.tile([P, 1, width], F32, name="inverse%d_top" % t)
                nc.vector.reciprocal(inverse[t][:, 0, :], levels[t][depth])
            for level in range(depth):
                for t in parts:
                    wider = keep.tile([P, 1, 2 * width], F32, name="wider", tag="inverse%d_%d" % (t, 2 * width))
                    nc.vector.tensor_tensor(
                        wider[:, 0, :].rearrange("p (a v) -> p a v", a=2),
                        levels[t][depth - 1 - level].rearrange("p (a v) -> p a v", a=2)[:, ::-1, :],
                        inverse[t][:].to_broadcast([P, 2, width]),
                        ALU.mult,
                    )
                    inverse[t] = wider
                width *= 2
            if batch:
                return {t: inverse[group[0]][:, 0, V * n : V * (n + 1)] for n, t in enumerate(group)}
            return {t: inverse[t][:, 0, :] for t in group}

        def make_tables(group, num, inverse):
            for tt, t in enumerate(group):
                nc.vector.scalar_tensor_tensor(
                    tables[t][:, :V], num[:, V * tt : V * (tt + 1)], size[:, t : t + 1], inverse[t], ALU.mult, ALU.mult
                )

        fetched = {}

        def fetch(t, chunk):
            r0, r1 = READER_CHUNKS[chunk]
            other = keep.tile([P, r1 - r0], F32, name="other%d_%d" % (t, chunk))
            nc.scalar.activation(other[:], tables[t][:].indirect(gs_t[:, r0 // 16 : r1 // 16]), ACT.Copy, scale=-0.6)
            own = tables[t][:].indirect(gt_t[:, r0 // 16 : r1 // 16])
            if (t, chunk) in SCALAR_BOTH:
                copied = keep.tile([P, r1 - r0], F32, name="own%d_%d" % (t, chunk))
                nc.scalar.activation(copied[:], own, ACT.Copy)
                own = copied[:]
            fetched[t, chunk] = (own, other)

        def subtract(t, chunk):
            own, other = fetched[t, chunk]
            nc.vector.tensor_tensor(diff[:, chunk, t, :], own, other[:], ALU.add)

        def finish(chunk):
            r0, r1 = FINISH_CHUNKS[chunk]
            width = r1 - r0
            half, c0 = divmod(r0, U // 2)
            hid = keep.tile([P, width, PACK], BF16, name="hid%d" % chunk, align_bytes=64)
            nc.vector.tensor_tensor(
                hid[:].rearrange("p (c i) t -> p c t i", i=4),
                diff[:, half, :, c0 : c0 + width].rearrange("p t (c i) -> p c t i", i=4),
                loc_s[:, :, r0:r1].rearrange("p t (c i) -> p c t i", i=4),
                ALU.max,
            )
            hid_codes = keep.tile([P, width], U32, name="hid_codes%d" % chunk, align_bytes=64)
            hid_scales = keep.tile([P, width], U8, name="hid_scales%d" % chunk, align_bytes=64)
            nc.vector.quantize_mx(
                out=hid_codes[:].bitcast(FP8X4), scales=hid_scales[:], in_=hid[:].rearrange("p r t -> p (r t)")
            )
            tag = ("gate_bank", "value_bank")[chunk % 2]
            bank = psum.tile([P, 2, width], F32, name=tag, bufs=BANKS[tag])
            for b in range(2):
                nc.tensor.matmul_mx(
                    out=bank[:, b, :],
                    lhsT=w3_codes[:, P * b : P * (b + 1)].bitcast(FP8X4),
                    lhsT_scale=w3_scales[:, P * b : P * (b + 1)],
                    rhs=hid_codes[:].bitcast(FP8X4),
                    rhs_scale=hid_scales[:],
                    start=True,
                    stop=True,
                )
            result = keep.tile([P, 2, width], F32, name="result%d" % chunk)
            copy = nc.vector.tensor_copy if r1 == U else nc.scalar.copy
            copy(out=result[:], in_=bank[:])
            nc.sync.dma_start(out=out[:, r0:r1].rearrange("(b m) r -> m b r", b=2), in_=result[:])

        gather_scales(0)
        gather_scales(1)
        gather_words(0)
        gather_words(1)
        rounded["w2"] = keep.tile([P, PACK, P, PACK], BF16, name="rounded", align_bytes=64)
        round_part(nc.scalar.copy, "w2", 0, 0, 64)
        round_part(nc.scalar.copy, "w2", 1, 0, W2_ON_SCALAR)
        round_part(nc.vector.tensor_copy, "w2", 1, W2_ON_SCALAR, 64)
        for t0, t1 in ((0, 1), (1, 4)):
            quantize_tiles("w2", t0, t1)

        split_unit()
        w3_ready = quantize_w3()
        rounded["w1"] = keep.tile([P, PACK, P, PACK], BF16, name="rounded_w1", align_bytes=64)
        round_part(nc.vector.tensor_copy, "w1", 0, W1_ON_SCALAR, 64)
        round_part(nc.vector.tensor_copy, "w1", 1, 0, 64)
        for t0, t1 in ((0, 1), (1, 4)):
            quantize_tiles("w1", t0, t1)
        w3_codes = keep.tile([P, N], U32, name="w3_codes", tag="raw_w1_1", align_bytes=64)
        pack_w3(w3_ready)
        inverse = {}
        groups = {0: [(0,)], 1: [(1,)], 3: [(2, 3)]}
        for s in range(PACK + 2):
            if s < PACK:
                for h in range(2):
                    make_weights(s, h)
            if 0 <= s - 1 < PACK:
                inverse.update(invert(sum_members(weight, (s - 1,), "den_bank")[:], (s - 1,), False, 2))
            if 0 <= s - 1 < PACK:
                for h in range(2):
                    weigh_values(s - 1, h)
            if 0 <= s - 2 < PACK:
                make_tables((s - 2,), sum_members(weighted, (s - 2,), "num_bank"), inverse)
        for r0, r1 in READER_CHUNKS:
            scale_loc(r0, r1)
        for chunk in range(2):
            for t in range(2):
                fetch(t, chunk)
        for chunk in range(2):
            for t in range(2, 4):
                fetch(t, chunk)
        diff = keep.tile([P, 2, PACK, U // 2], F32, name="diff", tag="inverse2_256")
        for chunk in range(2):
            for t in range(2):
                subtract(t, chunk)
        for chunk in range(2):
            for t in range(2, 4):
                subtract(t, chunk)
            for part in range(len(FINISH_CHUNKS)):
                if FINISH_CHUNKS[part][0] // 256 == chunk:
                    finish(part)
